import numpy as np
import ml_dtypes


def mxq(x, axis, fmt="e4m3"):
    dtype, down = {"e4m3": (ml_dtypes.float8_e4m3fn, 7), "e5m2": (ml_dtypes.float8_e5m2, 14)}[fmt]
    v = np.moveaxis(np.asarray(x, np.float32).astype(ml_dtypes.bfloat16).astype(np.float64), axis, -1)
    blocks = v.reshape(v.shape[:-1] + (-1, 32))
    amax = np.abs(blocks).max(-1, keepdims=True)
    byte = np.maximum(np.where(amax > 0, np.frexp(amax)[1] - 1 + 127, 0) - down, 1)
    scale = np.exp2(byte - 127.0)
    codes = (blocks / scale).astype(np.float32).astype(dtype).astype(np.float64)
    return np.moveaxis((codes * scale).reshape(v.shape), -1, axis)


WIDE = False


def mx_kscale(k):
    if not WIDE:
        return np.ones(k)
    levels = np.array([10, -10, 5, -5, 0])
    if k % 512:
        return np.exp2(np.random.permutation(np.resize(levels, k // 32))).repeat(32)
    a = np.empty((k // 512, 16))
    for p in range(k // 512):
        a[p, :8] = np.random.permutation(np.resize(levels, 8))
        for g in range(8):
            far = levels[np.abs(levels - a[p, g]) >= 10]
            a[p, g + 8] = far[np.random.randint(len(far))]
    return np.exp2(a.ravel()).repeat(32)


def f64(x):
    return np.asarray(x).astype(np.float64)


def striped(idx):
    return np.tile(np.asarray(idx).reshape(-1, 16).T, (8, 1)).astype(np.uint16)


def unstriped(offs):
    return offs[:16].T.reshape(-1).astype(np.int64)


def striped8(idx):
    return np.asarray(idx).reshape(8, -1, 16).transpose(0, 2, 1).reshape(128, -1).astype(np.uint16)


def unstriped8(offs):
    return offs.reshape(8, 16, -1).transpose(0, 2, 1).reshape(8, -1).astype(np.int64)


def pick8(x, idx, run):
    r = np.arange(len(x))
    return x[r[:, None], idx[r % (8 * run) // run]]


E2M1 = np.array([0.0, 0.5, 1.0, 1.5, 2.0, 3.0, 4.0, 6.0, -0.0, -0.5, -1.0, -1.5, -2.0, -3.0, -4.0, -6.0])


def pack_weight(w, fmt):
    k, n = w.shape
    w = f64(np.asarray(w, np.float32).astype(ml_dtypes.bfloat16)).reshape(k // 32, 32, n)
    amax = np.abs(w).max(1)
    if fmt == "e4m3":
        byte = np.frexp(amax)[1] - 1 + 127 - 7
    else:
        mant, ex = np.frexp(amax / 6.0)
        byte = np.where(mant > 0.5, ex, ex - 1) + 127
    byte = np.clip(np.where(amax > 0, byte, 1), 1, 254)
    scaled = (w * np.exp2(127.0 - byte)[:, None, :]).reshape(k, n).astype(np.float32)
    by_word = np.ascontiguousarray(scaled.reshape(k // 512, 128, 4, n).transpose(0, 1, 3, 2))
    if fmt == "e4m3":
        words = by_word.astype(ml_dtypes.float8_e4m3fn).view(np.uint8)
    else:
        c = by_word.astype(ml_dtypes.float4_e2m1fn).view(np.uint8) & 0xF
        words = (c[..., 0::2] | (c[..., 1::2] << 4)).reshape(k // 512, 128, 2 * n)
    return np.ascontiguousarray(words), np.ascontiguousarray(byte.astype(np.uint8).reshape(k // 512, 16, n))


def unpack_weight(words, scales, fmt):
    g, _, n = scales.shape
    words = np.ascontiguousarray(words).reshape(g, 128, n, -1)
    if fmt == "e4m3":
        vals = words.view(ml_dtypes.float8_e4m3fn).astype(np.float64)
    else:
        nib = np.empty((g, 128, n, 4), np.uint8)
        nib[..., 0::2] = words & 0xF
        nib[..., 1::2] = words >> 4
        vals = E2M1[nib]
    vals = vals * np.repeat(np.exp2(scales.astype(np.float64) - 127.0), 8, axis=1)[..., None]
    return vals.transpose(0, 1, 3, 2).reshape(g * 512, n)


def sigmoid(v):
    return 1.0 / (1.0 + np.exp(-v))


K, R, F, T, J, M, G = 512, 128, 512, 2048, 512, 256, 32


def setup_inputs():
    n = np.random.standard_normal
    idx = np.random.permutation(T)[:J]
    idx2 = np.stack([np.random.permutation(J)[:M] for _ in range(8)])
    fk = mx_kscale(K)
    ff = mx_kscale(F)
    tabp = pack_weight(n((K, T)) / fk[:, None], "e2m1")
    return {
        "tab_words": tabp[0],
        "tab_scales": tabp[1],
        "w1": (n((K, R)) * 1 / np.sqrt(K) * fk[:, None]).astype(np.float32),
        "gain": (np.random.uniform(0.5, 1.5, (R, 1))).astype(np.float32),
        "share": (np.random.uniform(0.4, 1.0, (R, 1))).astype(np.float32),
        "pb": (np.random.uniform(-0.5, 0.5, (1, M))).astype(np.float32),
        "wo": (n((F, R)) * 1 / np.sqrt(F) * ff[:, None]).astype(np.float32),
        "dy": (n((F, M)) / ff[:, None]).astype(np.float32),
        "og": (np.random.uniform(0.3, 1.0, (R, 1))).astype(np.float32),
        "base": (0.3 * n((R, J))).astype(np.float32),
        "offs": striped(idx),
        "offs2": striped8(idx2),
    }


def reference(tab_words, tab_scales, w1, gain, share, pb, wo, dy, og, base, offs, offs2):
    idx = unstriped(offs)
    idx2 = unstriped8(offs2)
    tabu = unpack_weight(tab_words, tab_scales, "e2m1")
    w1q = mxq(f64(w1), 0, "e4m3")
    tabidxg = tabu[:, idx]
    a = w1q.T @ tabidxg
    h0 = np.tanh(a)
    h1 = h0 * f64(gain)
    s = pick8(h1, idx2, 16) + f64(pb)
    m1 = s.reshape(R, G, M // G).mean(axis=2)
    mr = np.repeat(m1, M // G, axis=1)
    woq = mxq(f64(wo), 0, "e4m3")
    dyq = mxq(f64(dy), 0, "e4m3")
    c0 = woq.T @ dyq
    dmr = c0 * sigmoid(s - mr * f64(share)) * (-1.0) * f64(share)
    dm1 = dmr.reshape(R, G, M // G).sum(axis=2)
    e1 = dm1 / 8.0
    r1 = np.repeat(e1, M // G, axis=1)
    ds = c0 * sigmoid(s - mr * f64(share)) + r1
    s2 = np.zeros((R, J))
    s2[np.arange(R)[:, None], idx2[np.arange(R) % 128 // 16]] = ds
    dh0 = s2 * f64(gain)
    da = dh0 * (1.0 - np.square(h0))
    hda = da * 2.0
    hdh0 = hda * (1.0 - np.square(h0))
    hs2 = hdh0 * f64(gain)
    hds = pick8(hs2, idx2, 16)
    he1 = hds.reshape(R, G, M // G).sum(axis=2)
    hdm1 = he1 / 8.0
    r51 = np.repeat(hdm1, M // G, axis=1)
    hmr = hds * c0 * sigmoid(s - mr * f64(share)) * (1.0 - sigmoid(s - mr * f64(share))) * (-1.0) * f64(share) + r51 * f64(share) * (-1.0) * c0 * sigmoid(s - mr * f64(share)) * (1.0 - sigmoid(s - mr * f64(share))) * (-1.0) * f64(share)
    hm1 = hmr.reshape(R, G, M // G).sum(axis=2)
    e52 = hm1 / 8.0
    r52 = np.repeat(e52, M // G, axis=1)
    hs = hds * c0 * sigmoid(s - mr * f64(share)) * (1.0 - sigmoid(s - mr * f64(share))) + r51 * f64(share) * (-1.0) * c0 * sigmoid(s - mr * f64(share)) * (1.0 - sigmoid(s - mr * f64(share))) + r52
    s53 = np.zeros((R, J))
    s53[np.arange(R)[:, None], idx2[np.arange(R) % 128 // 16]] = hs
    hh0 = hda * dh0 * (-1.0) * h0 * 2.0 + s53 * f64(gain)
    ha = hh0 * (1.0 - np.square(h0))
    y = ha * f64(og) + f64(base)
    return y

@@ -1,0 +1,227 @@
+import math
+from contextlib import ExitStack
+
+import concourse.mybir as mybir
+from concourse.masks import make_identity
+
+F32 = mybir.dt.float32
+BF16 = mybir.dt.bfloat16
+I32 = mybir.dt.int32
+U32 = mybir.dt.uint32
+U16 = mybir.dt.uint16
+U8 = mybir.dt.uint8
+FP8X4 = mybir.dt.float8_e4m3fn_x4
+FP4X4 = mybir.dt.float4_e2m1fn_x4
+ACT = mybir.ActivationFunctionType
+MULT = mybir.AluOpType.mult
+ADD = mybir.AluOpType.add
+SUB = mybir.AluOpType.subtract
+AXIS_X = mybir.AxisListType.X
+
+P = 128
+PACK = 4
+K, R, F, T, J, M, GROUP = 512, 128, 512, 2048, 512, 256, 8
+LIST_ROWS = 16
+JH = J // 2
+MH = M // 2
+GH = MH // GROUP
+
+FLOPS = 2 * K * R * J + 2 * F * R * M
+
+
+def tile_attend_gpcpickcentred_kernel(tc, tab_words, tab_scales, w1, gain, share, pb, wo, dy, og, base, offs, offs2, out):
+    nc = tc.nc
+    halves = range(2)
+
+    with ExitStack() as ctx:
+        sb = ctx.enter_context(tc.tile_pool(name="sb", bufs=1))
+        ps = ctx.enter_context(tc.psum_pool(name="ps", bufs=1))
+
+        def tile(name, shape, dtype=F32):
+            return sb.tile(shape, dtype, name=name, align_bytes=64)
+
+        def jcols(h):
+            return slice(h * JH, (h + 1) * JH)
+
+        def mcols(h):
+            return slice(h * MH, (h + 1) * MH)
+
+        scales_t = tile("scales_t", [P, T], U8)
+        nc.vector.memset(scales_t[:].bitcast(I32), 0)
+        ident = tile("ident", [P, P])
+        nc.vector.memset(ident[:], 0.0)
+        s2 = tile("s2", [P, J])
+        nc.vector.memset(s2[:], 0.0)
+        s53 = tile("s53", [P, J])
+        nc.vector.memset(s53[:], 0.0)
+        make_identity(nc, ident[:], nomemset=True)
+
+        offs_t = tile("offs_t", [P, J // LIST_ROWS], U16)
+        nc.sync.dma_start(offs_t[:], offs)
+        scale_rows = tab_scales[0].bitcast(I32)
+        for r in range(4):
+            nc.scalar.dma_start(scales_t[:].bitcast(I32)[r:P:32, :], scale_rows[r:16:4, :])
+        words_t = tile("words_t", [P, T], U16)
+        nc.sync.dma_start(words_t[:].bitcast(I32), tab_words[0].bitcast(I32))
+        w1_raw = tile("w1_raw", [P, PACK, R])
+        nc.sync.dma_start(w1_raw[:], w1.rearrange("(p t) r -> p t r", t=PACK))
+        gain_t = tile("gain_t", [P, 1])
+        nc.sync.dma_start(gain_t[:], gain)
+        offs2_t = tile("offs2_t", [P, M // LIST_ROWS], U16)
+        nc.sync.dma_start(offs2_t[:], offs2)
+        pb_pairs = tile("pb_pairs", [P, 2])
+        nc.sync.dma_start(pb_pairs[:], pb[0].rearrange("(p c) -> p c", c=2))
+        wo_raw = tile("wo_raw", [P, PACK, R])
+        nc.sync.dma_start(wo_raw[:], wo.rearrange("(p t) r -> p t r", t=PACK))
+        dy_raw = tile("dy_raw", [P, PACK, M])
+        nc.sync.dma_start(dy_raw[:], dy.rearrange("(p t) m -> p t m", t=PACK))
+        share_t = tile("share_t", [P, 1])
+        nc.sync.dma_start(share_t[:], share)
+        og_t = tile("og_t", [P, 1])
+        nc.sync.dma_start(og_t[:], og)
+        base_t = tile("base_t", [P, J])
+        nc.sync.dma_start(base_t[:], base)
+
+        warm = tile("warm", [P, 1])
+        nc.scalar.activation(warm[:], s2[:, 0:1], ACT.Sigmoid)
+
+        def interleave(name, raw, cols):
+            width = cols.stop - cols.start
+            grouped = tile(name, [P, width, PACK], BF16)
+            nc.scalar.copy(grouped[:], raw[:, :, cols].rearrange("p t w -> p w t"))
+            return grouped
+
+        def quantize(name, grouped):
+            width = grouped.shape[1]
+            codes = tile(name + "_codes", [P, width], U32)
+            scales = tile(name + "_scales", [P, width], U8)
+            nc.vector.quantize_mx(codes[:].bitcast(FP8X4), scales[:], grouped[:].rearrange("p w t -> p (w t)"))
+            return codes, scales
+
+        def row_const(name, src, factor, other=None):
+            dst = tile(name, [P, 1])
+            if other is None:
+                nc.gpsimd.tensor_scalar(dst[:], src[:], factor, 0.0, MULT, ADD)
+            else:
+                nc.gpsimd.tensor_scalar(dst[:], src[:], other[:], factor, MULT, MULT)
+            return dst
+
+        jlist = [offs_t[:, h * JH // LIST_ROWS:(h + 1) * JH // LIST_ROWS] for h in halves]
+        mlist = [offs2_t[:, h * MH // LIST_ROWS:(h + 1) * MH // LIST_ROWS] for h in halves]
+        g_scales = [tile(f"g_scales{h}", [P, JH], U8) for h in halves]
+        g_words = [tile(f"g_words{h}", [P, JH], U16) for h in halves]
+        for h in halves:
+            nc.vector.tensor_copy(g_scales[h][:], scales_t[:].indirect(jlist[h]))
+        w1_bf = interleave("w1_bf", w1_raw, slice(0, R))
+        nc.vector.tensor_copy(g_words[0][:], words_t[:].indirect(jlist[0]))
+        w1_codes, w1_scales = quantize("w1", w1_bf)
+        nc.vector.tensor_copy(g_words[1][:], words_t[:].indirect(jlist[1]))
+
+        pb_ps = ps.tile([P, 2, P], F32, name="pb_ps")
+        for c in range(2):
+            nc.tensor.transpose(pb_ps[:, c, :], pb_pairs[:, c:c + 1].to_broadcast([P, P]), ident[:])
+        pb_all = tile("pb_all", [P, M])
+
+        h0 = tile("h0", [P, J])
+        h1 = tile("h1", [P, J])
+        for h in halves:
+            a_ps = ps.tile([P, JH], F32, name=f"a_ps{h}")
+            nc.tensor.matmul_mx(a_ps[:], lhsT=w1_codes[:].bitcast(FP8X4), lhsT_scale=w1_scales[:],
+                                rhs=g_words[h][:].bitcast(FP4X4), rhs_scale=g_scales[h][:], start=True, stop=True)
+            nc.scalar.activation(h0[:, jcols(h)], a_ps[:], ACT.Tanh)
+            nc.vector.tensor_scalar(h1[:, jcols(h)], h0[:, jcols(h)], gain_t[:], None, MULT)
+        nc.scalar.copy(pb_all[:].rearrange("p (n c) -> p n c", c=2), pb_ps[:].rearrange("p c n -> p n c"))
+
+        neg_share8 = row_const("neg_share8", share_t, -1.0 / GROUP)
+        pos_share8 = row_const("pos_share8", share_t, 1.0 / GROUP)
+        pos_rg = row_const("pos_rg", gain_t, math.sqrt(2.0))
+        neg_rg = row_const("neg_rg", gain_t, -math.sqrt(2.0))
+        pos_og = row_const("pos_og", og_t, 1.0, gain_t)
+        neg_og = row_const("neg_og", og_t, -1.0, gain_t)
+        neg_2og = row_const("neg_2og", og_t, -2.0)
+
+        wo_bf = interleave("wo_bf", wo_raw, slice(0, R))
+        dy_bf = [interleave(f"dy_bf{h}", dy_raw, mcols(h)) for h in halves]
+
+        def grouped(ap):
+            return ap.rearrange("p (g e) -> p g e", e=GROUP)
+
+        def spread(sums):
+            return sums[:].rearrange("p (g o) -> p g o", o=1).to_broadcast([P, GH, GROUP])
+
+        def group_sums(name, x):
+            sums = tile(name, [P, GH])
+            nc.vector.tensor_reduce(sums[:], grouped(x[:]), AXIS_X, ADD)
+            return sums
+
+        def mtiles(name):
+            return [tile(f"{name}{h}", [P, MH]) for h in halves]
+
+        s, z, sig, aa, r1, nb = (mtiles(n) for n in ("s", "z", "sig", "aa", "r1", "nb"))
+        for h in halves:
+            nc.vector.tensor_tensor(s[h][:], h1[:].indirect(mlist[h]), pb_all[:, mcols(h)], ADD)
+        s_sum = [group_sums(f"s_sum{h}", s[h]) for h in halves]
+        for h in halves:
+            nc.vector.scalar_tensor_tensor(grouped(z[h][:]), spread(s_sum[h]), neg_share8[:], grouped(s[h][:]), MULT, ADD)
+            nc.scalar.activation(sig[h][:], z[h][:], ACT.Sigmoid)
+        wo_codes, wo_scales = quantize("wo", wo_bf)
+        c0 = []
+        for h in halves:
+            dy_codes, dy_scales = quantize(f"dy{h}", dy_bf[h])
+            c_ps = ps.tile([P, MH], F32, name=f"c_ps{h}")
+            nc.tensor.matmul_mx(c_ps[:], lhsT=wo_codes[:].bitcast(FP8X4), lhsT_scale=wo_scales[:],
+                                rhs=dy_codes[:].bitcast(FP8X4), rhs_scale=dy_scales[:], start=True, stop=True)
+            c0.append(c_ps)
+        for h in halves:
+            nc.vector.tensor_tensor(aa[h][:], c0[h][:], sig[h][:], MULT)
+        a_sum = [group_sums(f"a_sum{h}", aa[h]) for h in halves]
+        for h in halves:
+            nc.vector.tensor_scalar(grouped(r1[h][:]), spread(a_sum[h]), neg_share8[:], None, MULT)
+        for h in halves:
+            nc.vector.tensor_tensor(s2[:].indirect(mlist[h]), aa[h][:], r1[h][:], ADD)
+
+        h0sq = tile("h0sq", [P, J])
+        nc.scalar.activation(h0sq[:], h0[:], ACT.Square)
+        wfac = tile("wfac", [P, J])
+        nc.scalar.activation(wfac[:], h0sq[:], ACT.Square, bias=pos_rg[:], scale=neg_rg[:])
+        s2sq = tile("s2sq", [P, J])
+        nc.scalar.activation(s2sq[:], s2[:], ACT.Square)
+        ufac = tile("ufac", [P, J])
+        nc.scalar.activation(ufac[:], h0sq[:], ACT.Identity, bias=pos_og[:], scale=neg_og[:])
+
+        hs2 = tile("hs2", [P, J])
+        for h in halves:
+            nc.vector.tensor_tensor(hs2[:, jcols(h)], s2[:, jcols(h)], wfac[:, jcols(h)], MULT)
+        hds, nz, pp, r52 = (mtiles(n) for n in ("hds", "nz", "pp", "r52"))
+        for h in halves:
+            nc.vector.tensor_copy(hds[h][:], hs2[:].indirect(mlist[h]))
+        for h in halves:
+            nc.vector.scalar_tensor_tensor(nb[h][:], sig[h][:], -1.0, aa[h][:], ADD, MULT)
+        h_sum = [group_sums(f"h_sum{h}", hds[h]) for h in halves]
+        for h in halves:
+            nc.vector.scalar_tensor_tensor(grouped(nz[h][:]), spread(h_sum[h]), pos_share8[:], grouped(hds[h][:]), MULT, SUB)
+        for h in halves:
+            nc.vector.tensor_tensor(pp[h][:], nz[h][:], nb[h][:], MULT)
+        p_sum = [group_sums(f"p_sum{h}", pp[h]) for h in halves]
+        for h in halves:
+            nc.vector.tensor_scalar(grouped(r52[h][:]), spread(p_sum[h]), neg_share8[:], None, MULT)
+        for h in halves:
+            nc.vector.tensor_tensor(s53[:].indirect(mlist[h]), pp[h][:], r52[h][:], ADD)
+
+        vfac = tile("vfac", [P, J])
+        term = tile("term", [P, J])
+        tb = tile("tb", [P, J])
+        f1 = tile("f1", [P, J])
+        res = tile("res", [P, J])
+        for h in halves:
+            nc.vector.tensor_tensor(f1[:, jcols(h)], s53[:, jcols(h)], ufac[:, jcols(h)], MULT)
+        for h in halves:
+            nc.vector.scalar_tensor_tensor(vfac[:, jcols(h)], h0[:, jcols(h)], neg_2og[:], wfac[:, jcols(h)], MULT, MULT)
+        for h in halves:
+            nc.vector.tensor_tensor(term[:, jcols(h)], vfac[:, jcols(h)], s2sq[:, jcols(h)], MULT)
+        for h in halves:
+            nc.vector.tensor_tensor(tb[:, jcols(h)], term[:, jcols(h)], base_t[:, jcols(h)], ADD)
+        for h in halves:
+            nc.vector.tensor_tensor(res[:, jcols(h)], f1[:, jcols(h)], tb[:, jcols(h)], ADD)
+            queue = nc.sync if h == 0 else nc.scalar
+            queue.dma_start(out[:, jcols(h)], res[:, jcols(h)])

@@ -23,6 +23,7 @@ PACK = 4
 K, R, F, T, J, M, GROUP = 512, 128, 512, 2048, 512, 256, 8
 LIST_ROWS = 16
 JH = J // 2
+JQ = J // 4
 MH = M // 2
 GH = MH // GROUP
 
@@ -37,8 +38,8 @@ def tile_attend_gpcpickcentred_kernel(tc, tab_words, tab_scales, w1, gain, share
         sb = ctx.enter_context(tc.tile_pool(name="sb", bufs=1))
         ps = ctx.enter_context(tc.psum_pool(name="ps", bufs=1))
 
-        def tile(name, shape, dtype=F32):
-            return sb.tile(shape, dtype, name=name, align_bytes=64)
+        def tile(name, shape, dtype=F32, tag=""):
+            return sb.tile(shape, dtype, name=name, tag=tag, align_bytes=64)
 
         def jcols(h):
             return slice(h * JH, (h + 1) * JH)
@@ -46,7 +47,7 @@ def tile_attend_gpcpickcentred_kernel(tc, tab_words, tab_scales, w1, gain, share
         def mcols(h):
             return slice(h * MH, (h + 1) * MH)
 
-        scales_t = tile("scales_t", [P, T], U8)
+        scales_t = tile("scales_t", [P, T], U8, "scales_dy")
         nc.vector.memset(scales_t[:].bitcast(I32), 0)
         ident = tile("ident", [P, P])
         nc.vector.memset(ident[:], 0.0)
@@ -54,27 +55,29 @@ def tile_attend_gpcpickcentred_kernel(tc, tab_words, tab_scales, w1, gain, share
         nc.vector.memset(s2[:], 0.0)
         s53 = tile("s53", [P, J])
         nc.vector.memset(s53[:], 0.0)
+        halfs = tile("halfs", [P, M])
+        nc.vector.memset(halfs[:], -0.5)
         make_identity(nc, ident[:], nomemset=True)
 
         offs_t = tile("offs_t", [P, J // LIST_ROWS], U16)
         nc.sync.dma_start(offs_t[:], offs)
-        scale_rows = tab_scales[0].bitcast(I32)
-        for r in range(4):
-            nc.scalar.dma_start(scales_t[:].bitcast(I32)[r:P:32, :], scale_rows[r:16:4, :])
         words_t = tile("words_t", [P, T], U16)
         nc.sync.dma_start(words_t[:].bitcast(I32), tab_words[0].bitcast(I32))
         w1_raw = tile("w1_raw", [P, PACK, R])
         nc.sync.dma_start(w1_raw[:], w1.rearrange("(p t) r -> p t r", t=PACK))
+        scale_rows = tab_scales[0].bitcast(I32)
+        for r in range(4):
+            nc.sync.dma_start(scales_t[:].bitcast(I32)[r:P:32, :], scale_rows[r:16:4, :])
+        pb_pairs = tile("pb_pairs", [P, 2], F32, "pb_w1")
+        nc.scalar.dma_start(pb_pairs[:], pb[0].rearrange("(p c) -> p c", c=2))
+        wo_raw = tile("wo_raw", [P, PACK, R], F32, "wo_h0")
+        nc.sync.dma_start(wo_raw[:], wo.rearrange("(p t) r -> p t r", t=PACK))
+        dy_raw = tile("dy_raw", [P, PACK, M])
+        nc.sync.dma_start(dy_raw[:], dy.rearrange("(p t) m -> p t m", t=PACK))
         gain_t = tile("gain_t", [P, 1])
         nc.sync.dma_start(gain_t[:], gain)
         offs2_t = tile("offs2_t", [P, M // LIST_ROWS], U16)
         nc.sync.dma_start(offs2_t[:], offs2)
-        pb_pairs = tile("pb_pairs", [P, 2])
-        nc.sync.dma_start(pb_pairs[:], pb[0].rearrange("(p c) -> p c", c=2))
-        wo_raw = tile("wo_raw", [P, PACK, R])
-        nc.sync.dma_start(wo_raw[:], wo.rearrange("(p t) r -> p t r", t=PACK))
-        dy_raw = tile("dy_raw", [P, PACK, M])
-        nc.sync.dma_start(dy_raw[:], dy.rearrange("(p t) m -> p t m", t=PACK))
         share_t = tile("share_t", [P, 1])
         nc.sync.dma_start(share_t[:], share)
         og_t = tile("og_t", [P, 1])
@@ -82,66 +85,18 @@ def tile_attend_gpcpickcentred_kernel(tc, tab_words, tab_scales, w1, gain, share
         base_t = tile("base_t", [P, J])
         nc.sync.dma_start(base_t[:], base)
 
-        warm = tile("warm", [P, 1])
-        nc.scalar.activation(warm[:], s2[:, 0:1], ACT.Sigmoid)
+        def interleave(copy, dst, raw):
+            copy(dst.rearrange("p (c i) t -> p c t i", i=4), raw.rearrange("p t (c i) -> p c t i", i=4))
 
-        def interleave(name, raw, cols):
-            width = cols.stop - cols.start
-            grouped = tile(name, [P, width, PACK], BF16)
-            nc.scalar.copy(grouped[:], raw[:, :, cols].rearrange("p t w -> p w t"))
-            return grouped
+        def scalar_cast(dst, src):
+            nc.scalar.activation(dst, src, ACT.Copy)
 
-        def quantize(name, grouped):
+        def quantize(name, grouped, tag=""):
             width = grouped.shape[1]
-            codes = tile(name + "_codes", [P, width], U32)
-            scales = tile(name + "_scales", [P, width], U8)
-            nc.vector.quantize_mx(codes[:].bitcast(FP8X4), scales[:], grouped[:].rearrange("p w t -> p (w t)"))
+            codes = tile(name + "_codes", [P, width], U32, tag)
+            scales = tile(name + "_scales", [P, width], U8, name + "_scales")
+            nc.vector.quantize_mx(codes[:].bitcast(FP8X4), scales[:], grouped.rearrange("p w t -> p (w t)"))
             return codes, scales
-
-        def row_const(name, src, factor, other=None):
-            dst = tile(name, [P, 1])
-            if other is None:
-                nc.gpsimd.tensor_scalar(dst[:], src[:], factor, 0.0, MULT, ADD)
-            else:
-                nc.gpsimd.tensor_scalar(dst[:], src[:], other[:], factor, MULT, MULT)
-            return dst
-
-        jlist = [offs_t[:, h * JH // LIST_ROWS:(h + 1) * JH // LIST_ROWS] for h in halves]
-        mlist = [offs2_t[:, h * MH // LIST_ROWS:(h + 1) * MH // LIST_ROWS] for h in halves]
-        g_scales = [tile(f"g_scales{h}", [P, JH], U8) for h in halves]
-        g_words = [tile(f"g_words{h}", [P, JH], U16) for h in halves]
-        for h in halves:
-            nc.vector.tensor_copy(g_scales[h][:], scales_t[:].indirect(jlist[h]))
-        w1_bf = interleave("w1_bf", w1_raw, slice(0, R))
-        nc.vector.tensor_copy(g_words[0][:], words_t[:].indirect(jlist[0]))
-        w1_codes, w1_scales = quantize("w1", w1_bf)
-        nc.vector.tensor_copy(g_words[1][:], words_t[:].indirect(jlist[1]))
-
-        pb_ps = ps.tile([P, 2, P], F32, name="pb_ps")
-        for c in range(2):
-            nc.tensor.transpose(pb_ps[:, c, :], pb_pairs[:, c:c + 1].to_broadcast([P, P]), ident[:])
-        pb_all = tile("pb_all", [P, M])
-
-        h0 = tile("h0", [P, J])
-        h1 = tile("h1", [P, J])
-        for h in halves:
-            a_ps = ps.tile([P, JH], F32, name=f"a_ps{h}")
-            nc.tensor.matmul_mx(a_ps[:], lhsT=w1_codes[:].bitcast(FP8X4), lhsT_scale=w1_scales[:],
-                                rhs=g_words[h][:].bitcast(FP4X4), rhs_scale=g_scales[h][:], start=True, stop=True)
-            nc.scalar.activation(h0[:, jcols(h)], a_ps[:], ACT.Tanh)
-            nc.vector.tensor_scalar(h1[:, jcols(h)], h0[:, jcols(h)], gain_t[:], None, MULT)
-        nc.scalar.copy(pb_all[:].rearrange("p (n c) -> p n c", c=2), pb_ps[:].rearrange("p c n -> p n c"))
-
-        neg_share8 = row_const("neg_share8", share_t, -1.0 / GROUP)
-        pos_share8 = row_const("pos_share8", share_t, 1.0 / GROUP)
-        pos_rg = row_const("pos_rg", gain_t, math.sqrt(2.0))
-        neg_rg = row_const("neg_rg", gain_t, -math.sqrt(2.0))
-        pos_og = row_const("pos_og", og_t, 1.0, gain_t)
-        neg_og = row_const("neg_og", og_t, -1.0, gain_t)
-        neg_2og = row_const("neg_2og", og_t, -2.0)
-
-        wo_bf = interleave("wo_bf", wo_raw, slice(0, R))
-        dy_bf = [interleave(f"dy_bf{h}", dy_raw, mcols(h)) for h in halves]
 
         def grouped(ap):
             return ap.rearrange("p (g e) -> p g e", e=GROUP)
@@ -149,78 +104,122 @@ def tile_attend_gpcpickcentred_kernel(tc, tab_words, tab_scales, w1, gain, share
         def spread(sums):
             return sums[:].rearrange("p (g o) -> p g o", o=1).to_broadcast([P, GH, GROUP])
 
-        def group_sums(name, x):
-            sums = tile(name, [P, GH])
-            nc.vector.tensor_reduce(sums[:], grouped(x[:]), AXIS_X, ADD)
+        def group_sums(name, x, tag=""):
+            sums = tile(name, [P, GH], F32, tag)
+            nc.vector.tensor_reduce(sums[:], grouped(x), AXIS_X, ADD)
             return sums
 
-        def mtiles(name):
-            return [tile(f"{name}{h}", [P, MH]) for h in halves]
+        def mtiles(name, tag=""):
+            whole = tile(name, [P, M], F32, tag)
+            return [whole[:, mcols(h)] for h in halves] + [whole[:]]
 
-        s, z, sig, aa, r1, nb = (mtiles(n) for n in ("s", "z", "sig", "aa", "r1", "nb"))
+        jlist = [offs_t[:, h * JH // LIST_ROWS:(h + 1) * JH // LIST_ROWS] for h in halves]
+        mlist = [offs2_t[:, h * MH // LIST_ROWS:(h + 1) * MH // LIST_ROWS] for h in halves]
+        g_words = tile("g_words", [P, J], U16, "words_gain")
+        nc.vector.tensor_copy(g_words[:], words_t[:].indirect(offs_t[:]))
+        w1_bf = tile("w1_bf", [P, R, PACK], BF16, "w1bf_scales")
+        interleave(scalar_cast, w1_bf[:], w1_raw[:])
+        pb_ps = ps.tile([P, 2, P], F32, name="pb_ps")
+        for c in range(2):
+            nc.tensor.transpose(pb_ps[:, c, :], pb_pairs[:, c:c + 1].to_broadcast([P, P]), ident[:])
+        pb_all = tile("pb_all", [P, M])
+        nc.scalar.copy(pb_all[:].rearrange("p (n c) -> p n c", c=2), pb_ps[:].rearrange("p c n -> p n c"))
+
+        g_scales = [tile("g_scales0", [P, JH], U8), tile("g_scales1", [P, JH], U8, "w1bf_scales")]
+        nc.vector.tensor_copy(g_scales[0][:], scales_t[:].indirect(jlist[0]))
+        w1_codes, w1_scales = quantize("w1", w1_bf[:], "pb_w1")
+        nc.vector.tensor_copy(g_scales[1][:], scales_t[:].indirect(jlist[1]))
+
+        wo_bf = tile("wo_bf", [P, R, PACK], BF16)
+        interleave(scalar_cast, wo_bf[:], wo_raw[:])
+        h0 = tile("h0", [P, J], F32, "wo_h0")
+        h1 = tile("h1", [P, J])
         for h in halves:
-            nc.vector.tensor_tensor(s[h][:], h1[:].indirect(mlist[h]), pb_all[:, mcols(h)], ADD)
-        s_sum = [group_sums(f"s_sum{h}", s[h]) for h in halves]
+            a_ps = ps.tile([P, JH], F32, name=f"a_ps{h}")
+            nc.tensor.matmul_mx(a_ps[:], lhsT=w1_codes[:].bitcast(FP8X4), lhsT_scale=w1_scales[:],
+                                rhs=g_words[:, jcols(h)].bitcast(FP4X4), rhs_scale=g_scales[h][:], start=True, stop=True)
+            nc.scalar.activation(h0[:, jcols(h)], a_ps[:], ACT.Tanh)
+
+        neg_gain = tile("neg_gain", [P, 1], F32, "words_gain")
+        nc.scalar.activation(neg_gain[:], gain_t[:], ACT.Copy, scale=-1.0)
+        dy_bf = tile("dy_bf", [P, M, PACK], BF16, "scales_dy")
         for h in halves:
-            nc.vector.scalar_tensor_tensor(grouped(z[h][:]), spread(s_sum[h]), neg_share8[:], grouped(s[h][:]), MULT, ADD)
-            nc.scalar.activation(sig[h][:], z[h][:], ACT.Sigmoid)
-        wo_codes, wo_scales = quantize("wo", wo_bf)
-        c0 = []
+            nc.vector.tensor_scalar(h1[:, jcols(h)], h0[:, jcols(h)], gain_t[:], None, MULT)
+        interleave(nc.vector.tensor_copy, dy_bf[:], dy_raw[:])
+        dy_codes, dy_scales = quantize("dy", dy_bf[:])
+        wo_codes, wo_scales = quantize("wo", wo_bf[:], "pb_w1")
+        c_ps = ps.tile([P, M], F32, name="c_ps")
+        nc.tensor.matmul_mx(c_ps[:], lhsT=wo_codes[:].bitcast(FP8X4), lhsT_scale=wo_scales[:],
+                            rhs=dy_codes[:].bitcast(FP8X4), rhs_scale=dy_scales[:], start=True, stop=True)
+
+        s, z, sig, aa, r1 = (mtiles(n) for n in ("s", "z", "sig", "aa", "r1"))
         for h in halves:
-            dy_codes, dy_scales = quantize(f"dy{h}", dy_bf[h])
-            c_ps = ps.tile([P, MH], F32, name=f"c_ps{h}")
-            nc.tensor.matmul_mx(c_ps[:], lhsT=wo_codes[:].bitcast(FP8X4), lhsT_scale=wo_scales[:],
-                                rhs=dy_codes[:].bitcast(FP8X4), rhs_scale=dy_scales[:], start=True, stop=True)
-            c0.append(c_ps)
+            nc.vector.tensor_tensor(s[h], h1[:].indirect(mlist[h]), pb_all[:, mcols(h)], ADD)
+        s_sum = [group_sums("s_sum0", s[0]), group_sums("s_sum1", s[1], "sum_v")]
+        share8 = tile("share8", [P, 1], F32, "w1_scales")
+        nc.vector.tensor_scalar(share8[:], share_t[:], 1.0 / GROUP, None, MULT)
         for h in halves:
-            nc.vector.tensor_tensor(aa[h][:], c0[h][:], sig[h][:], MULT)
-        a_sum = [group_sums(f"a_sum{h}", aa[h]) for h in halves]
-        for h in halves:
-            nc.vector.tensor_scalar(grouped(r1[h][:]), spread(a_sum[h]), neg_share8[:], None, MULT)
-        for h in halves:
-            nc.vector.tensor_tensor(s2[:].indirect(mlist[h]), aa[h][:], r1[h][:], ADD)
+            nc.vector.scalar_tensor_tensor(grouped(z[h]), spread(s_sum[h]), share8[:], grouped(s[h]), MULT, SUB)
+            nc.scalar.activation(sig[h], z[h], ACT.Tanh, scale=-0.5)
 
         h0sq = tile("h0sq", [P, J])
         nc.scalar.activation(h0sq[:], h0[:], ACT.Square)
+        dfac = tile("dfac", [P, J])
+        nc.scalar.activation(dfac[:], h0sq[:], ACT.Identity, bias=gain_t[:], scale=neg_gain[:])
         wfac = tile("wfac", [P, J])
-        nc.scalar.activation(wfac[:], h0sq[:], ACT.Square, bias=pos_rg[:], scale=neg_rg[:])
-        s2sq = tile("s2sq", [P, J])
-        nc.scalar.activation(s2sq[:], s2[:], ACT.Square)
-        ufac = tile("ufac", [P, J])
-        nc.scalar.activation(ufac[:], h0sq[:], ACT.Identity, bias=pos_og[:], scale=neg_og[:])
+        nc.scalar.activation(wfac[:], dfac[:], ACT.Square, scale=math.sqrt(2.0))
 
-        hs2 = tile("hs2", [P, J])
-        for h in halves:
-            nc.vector.tensor_tensor(hs2[:, jcols(h)], s2[:, jcols(h)], wfac[:, jcols(h)], MULT)
-        hds, nz, pp, r52 = (mtiles(n) for n in ("hds", "nz", "pp", "r52"))
-        for h in halves:
-            nc.vector.tensor_copy(hds[h][:], hs2[:].indirect(mlist[h]))
-        for h in halves:
-            nc.vector.scalar_tensor_tensor(nb[h][:], sig[h][:], -1.0, aa[h][:], ADD, MULT)
-        h_sum = [group_sums(f"h_sum{h}", hds[h]) for h in halves]
-        for h in halves:
-            nc.vector.scalar_tensor_tensor(grouped(nz[h][:]), spread(h_sum[h]), pos_share8[:], grouped(hds[h][:]), MULT, SUB)
-        for h in halves:
-            nc.vector.tensor_tensor(pp[h][:], nz[h][:], nb[h][:], MULT)
-        p_sum = [group_sums(f"p_sum{h}", pp[h]) for h in halves]
-        for h in halves:
-            nc.vector.tensor_scalar(grouped(r52[h][:]), spread(p_sum[h]), neg_share8[:], None, MULT)
-        for h in halves:
-            nc.vector.tensor_tensor(s53[:].indirect(mlist[h]), pp[h][:], r52[h][:], ADD)
-
-        vfac = tile("vfac", [P, J])
+        vfac = tile("vfac", [P, J], F32, "sum_v")
         term = tile("term", [P, J])
-        tb = tile("tb", [P, J])
         f1 = tile("f1", [P, J])
         res = tile("res", [P, J])
+        s2sq = tile("s2sq", [P, J])
+
+
+        def qcols(q):
+            return slice(q * JQ, (q + 1) * JQ)
+
+        def v_part(q):
+            nc.vector.scalar_tensor_tensor(vfac[:, qcols(q)], h0[:, qcols(q)], -2.0, wfac[:, qcols(q)], MULT, MULT)
+
+        def term_part(q):
+            nc.vector.scalar_tensor_tensor(term[:, qcols(q)], vfac[:, qcols(q)], og_t[:], s2sq[:, qcols(q)], MULT, MULT)
+
         for h in halves:
-            nc.vector.tensor_tensor(f1[:, jcols(h)], s53[:, jcols(h)], ufac[:, jcols(h)], MULT)
+            nc.vector.scalar_tensor_tensor(aa[h], sig[h], 1.0, c_ps[:, mcols(h)], ADD, MULT)
+        a_sum = [group_sums("a_sum0", aa[0]), group_sums("a_sum1", aa[1])]
         for h in halves:
-            nc.vector.scalar_tensor_tensor(vfac[:, jcols(h)], h0[:, jcols(h)], neg_2og[:], wfac[:, jcols(h)], MULT, MULT)
+            nc.vector.scalar_tensor_tensor(grouped(r1[h]), spread(a_sum[h]), share8[:], grouped(aa[h]), MULT, SUB)
+        nc.vector.tensor_tensor(s2[:].indirect(offs2_t[:]), r1[2], halfs[:], MULT)
+        nc.scalar.activation(s2sq[:], s2[:], ACT.Square)
+
+        hs2 = tile("hs2", [P, J])
+        nc.vector.tensor_tensor(hs2[:], s2[:], wfac[:], MULT)
+        hds, nz, pp, r52 = (mtiles(n) for n in ("hds", "nz", "pp", "r52"))
         for h in halves:
-            nc.vector.tensor_tensor(term[:, jcols(h)], vfac[:, jcols(h)], s2sq[:, jcols(h)], MULT)
+            nc.vector.tensor_copy(hds[h], hs2[:].indirect(mlist[h]))
+        h_sum = [group_sums(f"h_sum{h}", hds[h]) for h in halves]
         for h in halves:
-            nc.vector.tensor_tensor(tb[:, jcols(h)], term[:, jcols(h)], base_t[:, jcols(h)], ADD)
+            nc.vector.scalar_tensor_tensor(grouped(nz[h]), spread(h_sum[h]), share8[:], grouped(hds[h]), MULT, SUB)
+        nb = mtiles("nb")
+        for h in halves:
+            nc.vector.scalar_tensor_tensor(nb[h], sig[h], -1.0, aa[h], ADD, MULT)
+        for h in halves:
+            nc.vector.scalar_tensor_tensor(pp[h], nz[h], 0.25, nb[h], MULT, MULT)
+        p_sum = [group_sums("p_sum0", pp[0]), group_sums("p_sum1", pp[1])]
+        for h in halves:
+            nc.vector.tensor_scalar(grouped(r52[h]), spread(p_sum[h]), share_t[:], -1.0 / GROUP, MULT, MULT)
+        nc.vector.tensor_tensor(s53[:].indirect(offs2_t[:]), pp[2], r52[2], ADD)
+
+        for h in halves:
+            nc.vector.scalar_tensor_tensor(f1[:, jcols(h)], s53[:, jcols(h)], og_t[:], dfac[:, jcols(h)], MULT, MULT)
+        for q in range(4):
+            v_part(q)
+        for q in range(4):
+            term_part(q)
+        tb = tile("tb", [P, J])
+        for q in range(4):
+            nc.vector.tensor_tensor(tb[:, qcols(q)], term[:, qcols(q)], base_t[:, qcols(q)], ADD)
         for h in halves:
             nc.vector.tensor_tensor(res[:, jcols(h)], f1[:, jcols(h)], tb[:, jcols(h)], ADD)
             queue = nc.sync if h == 0 else nc.scalar

@@ -20,12 +20,14 @@ AXIS_X = mybir.AxisListType.X
 
 P = 128
 PACK = 4
-K, R, F, T, J, M, GROUP = 512, 128, 512, 2048, 512, 256, 8
+K, R, F, T, J, M = 512, 128, 512, 2048, 512, 256
+GROUP = 8
 LIST_ROWS = 16
-JH = J // 2
-JQ = J // 4
-MH = M // 2
-GH = MH // GROUP
+SCALE_ROWS = 16
+QUADRANT = 32
+LINE = 4
+PICK_PARTS = 4
+SLOT_PARTS = 4
 
 FLOPS = 2 * K * R * J + 2 * F * R * M
 
@@ -33,6 +35,24 @@ FLOPS = 2 * K * R * J + 2 * F * R * M
 def tile_attend_gpcpickcentred_kernel(tc, tab_words, tab_scales, w1, gain, share, pb, wo, dy, og, base, offs, offs2, out):
     nc = tc.nc
     halves = range(2)
+    pick_parts = range(PICK_PARTS)
+    slot_parts = range(SLOT_PARTS)
+    part_groups = M // PICK_PARTS // GROUP
+
+    def piece(width, count, i):
+        return slice(i * width // count, (i + 1) * width // count)
+
+    def slot_half(h):
+        return piece(J, 2, h)
+
+    def slot_part(q):
+        return piece(J, SLOT_PARTS, q)
+
+    def pick_half(h):
+        return piece(M, 2, h)
+
+    def pick_part(q):
+        return piece(M, PICK_PARTS, q)
 
     with ExitStack() as ctx:
         sb = ctx.enter_context(tc.tile_pool(name="sb", bufs=1))
@@ -41,13 +61,7 @@ def tile_attend_gpcpickcentred_kernel(tc, tab_words, tab_scales, w1, gain, share
         def tile(name, shape, dtype=F32, tag=""):
             return sb.tile(shape, dtype, name=name, tag=tag, align_bytes=64)
 
-        def jcols(h):
-            return slice(h * JH, (h + 1) * JH)
-
-        def mcols(h):
-            return slice(h * MH, (h + 1) * MH)
-
-        scales_t = tile("scales_t", [P, T], U8, "scales_dy")
+        scales_t = tile("scales_t", [P, T], U8, "scales_then_dy")
         nc.vector.memset(scales_t[:].bitcast(I32), 0)
         ident = tile("ident", [P, P])
         nc.vector.memset(ident[:], 0.0)
@@ -55,8 +69,8 @@ def tile_attend_gpcpickcentred_kernel(tc, tab_words, tab_scales, w1, gain, share
         nc.vector.memset(s2[:], 0.0)
         s53 = tile("s53", [P, J])
         nc.vector.memset(s53[:], 0.0)
-        halfs = tile("halfs", [P, M])
-        nc.vector.memset(halfs[:], -0.5)
+        neg_half = tile("neg_half", [P, M])
+        nc.vector.memset(neg_half[:], -0.5)
         make_identity(nc, ident[:], nomemset=True)
 
         offs_t = tile("offs_t", [P, J // LIST_ROWS], U16)
@@ -66,11 +80,11 @@ def tile_attend_gpcpickcentred_kernel(tc, tab_words, tab_scales, w1, gain, share
         w1_raw = tile("w1_raw", [P, PACK, R])
         nc.sync.dma_start(w1_raw[:], w1.rearrange("(p t) r -> p t r", t=PACK))
         scale_rows = tab_scales[0].bitcast(I32)
-        for r in range(4):
-            nc.sync.dma_start(scales_t[:].bitcast(I32)[r:P:32, :], scale_rows[r:16:4, :])
-        pb_pairs = tile("pb_pairs", [P, 2], F32, "pb_w1")
+        for i in range(4):
+            nc.sync.dma_start(scales_t[:].bitcast(I32)[i:P:QUADRANT, :], scale_rows[i:SCALE_ROWS:4, :])
+        pb_pairs = tile("pb_pairs", [P, 2], F32, "pb_then_w1_then_wo")
         nc.scalar.dma_start(pb_pairs[:], pb[0].rearrange("(p c) -> p c", c=2))
-        wo_raw = tile("wo_raw", [P, PACK, R], F32, "wo_h0")
+        wo_raw = tile("wo_raw", [P, PACK, R], F32, "wo_then_h0")
         nc.sync.dma_start(wo_raw[:], wo.rearrange("(p t) r -> p t r", t=PACK))
         dy_raw = tile("dy_raw", [P, PACK, M])
         nc.sync.dma_start(dy_raw[:], dy.rearrange("(p t) m -> p t m", t=PACK))
@@ -86,141 +100,149 @@ def tile_attend_gpcpickcentred_kernel(tc, tab_words, tab_scales, w1, gain, share
         nc.sync.dma_start(base_t[:], base)
 
         def interleave(copy, dst, raw):
-            copy(dst.rearrange("p (c i) t -> p c t i", i=4), raw.rearrange("p t (c i) -> p c t i", i=4))
+            copy(dst.rearrange("p (c i) t -> p c t i", i=LINE), raw.rearrange("p t (c i) -> p c t i", i=LINE))
 
         def scalar_cast(dst, src):
             nc.scalar.activation(dst, src, ACT.Copy)
 
-        def quantize(name, grouped, tag=""):
-            width = grouped.shape[1]
-            codes = tile(name + "_codes", [P, width], U32, tag)
-            scales = tile(name + "_scales", [P, width], U8, name + "_scales")
-            nc.vector.quantize_mx(codes[:].bitcast(FP8X4), scales[:], grouped.rearrange("p w t -> p (w t)"))
+        def quantize(name, interleaved, codes_tag="", scales_tag=""):
+            width = interleaved.shape[1]
+            codes = tile(name + "_codes", [P, width], U32, codes_tag)
+            scales = tile(name + "_scales", [P, width], U8, scales_tag)
+            nc.vector.quantize_mx(codes[:].bitcast(FP8X4), scales[:], interleaved.rearrange("p w t -> p (w t)"))
             return codes, scales
 
-        def grouped(ap):
+        def by_group(ap):
             return ap.rearrange("p (g e) -> p g e", e=GROUP)
 
         def spread(sums):
-            return sums[:].rearrange("p (g o) -> p g o", o=1).to_broadcast([P, GH, GROUP])
+            return sums[:].rearrange("p (g o) -> p g o", o=1).to_broadcast([P, part_groups, GROUP])
 
-        def group_sums(name, x, tag=""):
-            sums = tile(name, [P, GH], F32, tag)
-            nc.vector.tensor_reduce(sums[:], grouped(x), AXIS_X, ADD)
+        def group_sums(name, x, last_tag=""):
+            sums = []
+            for q in pick_parts:
+                part = tile(f"{name}{q}", [P, part_groups], F32, last_tag if q == PICK_PARTS - 1 else "")
+                nc.vector.tensor_reduce(part[:], by_group(x[:, pick_part(q)]), AXIS_X, ADD)
+                sums.append(part)
             return sums
 
-        def mtiles(name, tag=""):
-            whole = tile(name, [P, M], F32, tag)
-            return [whole[:, mcols(h)] for h in halves] + [whole[:]]
+        def neg_centre(dst, x, sums, q):
+            cols = pick_part(q)
+            nc.vector.scalar_tensor_tensor(by_group(dst[:, cols]), spread(sums[q]), share8[:], by_group(x[:, cols]), MULT, SUB)
 
-        jlist = [offs_t[:, h * JH // LIST_ROWS:(h + 1) * JH // LIST_ROWS] for h in halves]
-        mlist = [offs2_t[:, h * MH // LIST_ROWS:(h + 1) * MH // LIST_ROWS] for h in halves]
-        g_words = tile("g_words", [P, J], U16, "words_gain")
+        slot_list = [offs_t[:, piece(J // LIST_ROWS, 2, h)] for h in halves]
+        pick_list = [offs2_t[:, piece(M // LIST_ROWS, 2, h)] for h in halves]
+        g_words = tile("g_words", [P, J], U16, "words_then_gain")
         nc.vector.tensor_copy(g_words[:], words_t[:].indirect(offs_t[:]))
-        w1_bf = tile("w1_bf", [P, R, PACK], BF16, "w1bf_scales")
+        w1_bf = tile("w1_bf", [P, R, PACK], BF16, "w1_then_scales")
         interleave(scalar_cast, w1_bf[:], w1_raw[:])
+
         pb_ps = ps.tile([P, 2, P], F32, name="pb_ps")
         for c in range(2):
             nc.tensor.transpose(pb_ps[:, c, :], pb_pairs[:, c:c + 1].to_broadcast([P, P]), ident[:])
         pb_all = tile("pb_all", [P, M])
         nc.scalar.copy(pb_all[:].rearrange("p (n c) -> p n c", c=2), pb_ps[:].rearrange("p c n -> p n c"))
 
-        g_scales = [tile("g_scales0", [P, JH], U8), tile("g_scales1", [P, JH], U8, "w1bf_scales")]
-        nc.vector.tensor_copy(g_scales[0][:], scales_t[:].indirect(jlist[0]))
-        w1_codes, w1_scales = quantize("w1", w1_bf[:], "pb_w1")
-        nc.vector.tensor_copy(g_scales[1][:], scales_t[:].indirect(jlist[1]))
+        g_scales = [tile("g_scales0", [P, J // 2], U8), tile("g_scales1", [P, J // 2], U8, "w1_then_scales")]
+        nc.vector.tensor_copy(g_scales[0][:], scales_t[:].indirect(slot_list[0]))
+        w1_codes, w1_scales = quantize("w1", w1_bf[:], "pb_then_w1_then_wo", "w1_then_share")
+        nc.vector.tensor_copy(g_scales[1][:], scales_t[:].indirect(slot_list[1]))
 
         wo_bf = tile("wo_bf", [P, R, PACK], BF16)
         interleave(scalar_cast, wo_bf[:], wo_raw[:])
-        h0 = tile("h0", [P, J], F32, "wo_h0")
+        h0 = tile("h0", [P, J], F32, "wo_then_h0")
         h1 = tile("h1", [P, J])
         for h in halves:
-            a_ps = ps.tile([P, JH], F32, name=f"a_ps{h}")
+            a_ps = ps.tile([P, J // 2], F32, name=f"a_ps{h}")
             nc.tensor.matmul_mx(a_ps[:], lhsT=w1_codes[:].bitcast(FP8X4), lhsT_scale=w1_scales[:],
-                                rhs=g_words[:, jcols(h)].bitcast(FP4X4), rhs_scale=g_scales[h][:], start=True, stop=True)
-            nc.scalar.activation(h0[:, jcols(h)], a_ps[:], ACT.Tanh)
-
-        neg_gain = tile("neg_gain", [P, 1], F32, "words_gain")
+                                rhs=g_words[:, slot_half(h)].bitcast(FP4X4), rhs_scale=g_scales[h][:], start=True, stop=True)
+            nc.scalar.activation(h0[:, slot_half(h)], a_ps[:], ACT.Tanh)
+        neg_gain = tile("neg_gain", [P, 1], F32, "words_then_gain")
         nc.scalar.activation(neg_gain[:], gain_t[:], ACT.Copy, scale=-1.0)
-        dy_bf = tile("dy_bf", [P, M, PACK], BF16, "scales_dy")
+        dy_bf = tile("dy_bf", [P, M, PACK], BF16, "scales_then_dy")
         for h in halves:
-            nc.vector.tensor_scalar(h1[:, jcols(h)], h0[:, jcols(h)], gain_t[:], None, MULT)
+            nc.vector.tensor_scalar(h1[:, slot_half(h)], h0[:, slot_half(h)], gain_t[:], None, MULT)
         interleave(nc.vector.tensor_copy, dy_bf[:], dy_raw[:])
         dy_codes, dy_scales = quantize("dy", dy_bf[:])
-        wo_codes, wo_scales = quantize("wo", wo_bf[:], "pb_w1")
-        c_ps = ps.tile([P, M], F32, name="c_ps")
-        nc.tensor.matmul_mx(c_ps[:], lhsT=wo_codes[:].bitcast(FP8X4), lhsT_scale=wo_scales[:],
+        wo_codes, wo_scales = quantize("wo", wo_bf[:], "pb_then_w1_then_wo")
+        c0 = ps.tile([P, M], F32, name="c0")
+        nc.tensor.matmul_mx(c0[:], lhsT=wo_codes[:].bitcast(FP8X4), lhsT_scale=wo_scales[:],
                             rhs=dy_codes[:].bitcast(FP8X4), rhs_scale=dy_scales[:], start=True, stop=True)
 
-        s, z, sig, aa, r1 = (mtiles(n) for n in ("s", "z", "sig", "aa", "r1"))
+        s, neg_z, th, two_cs, neg_two_ds = (tile(n, [P, M]) for n in ("s", "neg_z", "th", "two_cs", "neg_two_ds"))
         for h in halves:
-            nc.vector.tensor_tensor(s[h], h1[:].indirect(mlist[h]), pb_all[:, mcols(h)], ADD)
-        s_sum = [group_sums("s_sum0", s[0]), group_sums("s_sum1", s[1], "sum_v")]
-        share8 = tile("share8", [P, 1], F32, "w1_scales")
+            nc.vector.tensor_tensor(s[:, pick_half(h)], h1[:].indirect(pick_list[h]), pb_all[:, pick_half(h)], ADD)
+        s_sums = group_sums("s_sum", s, "sum_then_v")
+        share8 = tile("share8", [P, 1], F32, "w1_then_share")
         nc.vector.tensor_scalar(share8[:], share_t[:], 1.0 / GROUP, None, MULT)
-        for h in halves:
-            nc.vector.scalar_tensor_tensor(grouped(z[h]), spread(s_sum[h]), share8[:], grouped(s[h]), MULT, SUB)
-            nc.scalar.activation(sig[h], z[h], ACT.Tanh, scale=-0.5)
+        for q in pick_parts:
+            neg_centre(neg_z, s, s_sums, q)
+            nc.scalar.activation(th[:, pick_part(q)], neg_z[:, pick_part(q)], ACT.Tanh, scale=-0.5)
 
-        h0sq = tile("h0sq", [P, J])
-        nc.scalar.activation(h0sq[:], h0[:], ACT.Square)
-        dfac = tile("dfac", [P, J])
-        nc.scalar.activation(dfac[:], h0sq[:], ACT.Identity, bias=gain_t[:], scale=neg_gain[:])
-        wfac = tile("wfac", [P, J])
-        nc.scalar.activation(wfac[:], dfac[:], ACT.Square, scale=math.sqrt(2.0))
+        h0_sq = tile("h0_sq", [P, J])
+        nc.scalar.activation(h0_sq[:], h0[:], ACT.Square)
+        gain_u = tile("gain_u", [P, J])
+        nc.scalar.activation(gain_u[:], h0_sq[:], ACT.Identity, bias=gain_t[:], scale=neg_gain[:])
+        two_gu2 = tile("two_gu2", [P, J])
+        nc.scalar.activation(two_gu2[:], gain_u[:], ACT.Square, scale=math.sqrt(2.0))
 
-        vfac = tile("vfac", [P, J], F32, "sum_v")
-        term = tile("term", [P, J])
-        f1 = tile("f1", [P, J])
-        res = tile("res", [P, J])
-        s2sq = tile("s2sq", [P, J])
-
-
-        def qcols(q):
-            return slice(q * JQ, (q + 1) * JQ)
-
-        def v_part(q):
-            nc.vector.scalar_tensor_tensor(vfac[:, qcols(q)], h0[:, qcols(q)], -2.0, wfac[:, qcols(q)], MULT, MULT)
-
-        def term_part(q):
-            nc.vector.scalar_tensor_tensor(term[:, qcols(q)], vfac[:, qcols(q)], og_t[:], s2sq[:, qcols(q)], MULT, MULT)
-
-        for h in halves:
-            nc.vector.scalar_tensor_tensor(aa[h], sig[h], 1.0, c_ps[:, mcols(h)], ADD, MULT)
-        a_sum = [group_sums("a_sum0", aa[0]), group_sums("a_sum1", aa[1])]
-        for h in halves:
-            nc.vector.scalar_tensor_tensor(grouped(r1[h]), spread(a_sum[h]), share8[:], grouped(aa[h]), MULT, SUB)
-        nc.vector.tensor_tensor(s2[:].indirect(offs2_t[:]), r1[2], halfs[:], MULT)
-        nc.scalar.activation(s2sq[:], s2[:], ACT.Square)
+        for q in pick_parts:
+            cols = pick_part(q)
+            nc.vector.scalar_tensor_tensor(two_cs[:, cols], th[:, cols], 1.0, c0[:, cols], ADD, MULT)
+        cs_sums = group_sums("cs_sum", two_cs)
+        for q in pick_parts:
+            neg_centre(neg_two_ds, two_cs, cs_sums, q)
+        nc.vector.tensor_tensor(s2[:].indirect(offs2_t[:]), neg_two_ds[:], neg_half[:], MULT)
+        s2_sq = tile("s2_sq", [P, J])
+        nc.scalar.activation(s2_sq[:], s2[:], ACT.Square)
 
         hs2 = tile("hs2", [P, J])
-        nc.vector.tensor_tensor(hs2[:], s2[:], wfac[:], MULT)
-        hds, nz, pp, r52 = (mtiles(n) for n in ("hds", "nz", "pp", "r52"))
+        nc.vector.tensor_tensor(hs2[:], s2[:], two_gu2[:], MULT)
+        hds, neg_ch, curved, r52 = (tile(n, [P, M]) for n in ("hds", "neg_ch", "curved", "r52"))
         for h in halves:
-            nc.vector.tensor_copy(hds[h], hs2[:].indirect(mlist[h]))
-        h_sum = [group_sums(f"h_sum{h}", hds[h]) for h in halves]
+            nc.vector.tensor_copy(hds[:, pick_half(h)], hs2[:].indirect(pick_list[h]))
+        hds_sums = group_sums("hds_sum", hds)
+        for q in pick_parts:
+            neg_centre(neg_ch, hds, hds_sums, q)
+        neg_four_slope = tile("neg_four_slope", [P, M])
         for h in halves:
-            nc.vector.scalar_tensor_tensor(grouped(nz[h]), spread(h_sum[h]), share8[:], grouped(hds[h]), MULT, SUB)
-        nb = mtiles("nb")
-        for h in halves:
-            nc.vector.scalar_tensor_tensor(nb[h], sig[h], -1.0, aa[h], ADD, MULT)
-        for h in halves:
-            nc.vector.scalar_tensor_tensor(pp[h], nz[h], 0.25, nb[h], MULT, MULT)
-        p_sum = [group_sums("p_sum0", pp[0]), group_sums("p_sum1", pp[1])]
-        for h in halves:
-            nc.vector.tensor_scalar(grouped(r52[h]), spread(p_sum[h]), share_t[:], -1.0 / GROUP, MULT, MULT)
-        nc.vector.tensor_tensor(s53[:].indirect(offs2_t[:]), pp[2], r52[2], ADD)
+            cols = pick_half(h)
+            nc.vector.scalar_tensor_tensor(neg_four_slope[:, cols], th[:, cols], -1.0, two_cs[:, cols], ADD, MULT)
+        for q in pick_parts:
+            cols = pick_part(q)
+            nc.vector.scalar_tensor_tensor(curved[:, cols], neg_ch[:, cols], 0.25, neg_four_slope[:, cols], MULT, MULT)
+        curved_sums = group_sums("curved_sum", curved)
+        for q in pick_parts:
+            nc.vector.tensor_scalar(by_group(r52[:, pick_part(q)]), spread(curved_sums[q]), share_t[:], -1.0 / GROUP, MULT, MULT)
+        nc.vector.tensor_tensor(s53[:].indirect(offs2_t[:]), curved[:], r52[:], ADD)
 
+        linear = tile("linear", [P, J])
         for h in halves:
-            nc.vector.scalar_tensor_tensor(f1[:, jcols(h)], s53[:, jcols(h)], og_t[:], dfac[:, jcols(h)], MULT, MULT)
-        for q in range(4):
-            v_part(q)
-        for q in range(4):
-            term_part(q)
-        tb = tile("tb", [P, J])
-        for q in range(4):
-            nc.vector.tensor_tensor(tb[:, qcols(q)], term[:, qcols(q)], base_t[:, qcols(q)], ADD)
+            cols = slot_half(h)
+            nc.vector.scalar_tensor_tensor(linear[:, cols], s53[:, cols], og_t[:], gain_u[:, cols], MULT, MULT)
+        v = tile("v", [P, J], F32, "sum_then_v")
+        for q in slot_parts:
+            cols = slot_part(q)
+            nc.vector.scalar_tensor_tensor(v[:, cols], h0[:, cols], -2.0, two_gu2[:, cols], MULT, MULT)
+        square = tile("square", [P, J])
+        for q in slot_parts:
+            cols = slot_part(q)
+            nc.vector.scalar_tensor_tensor(square[:, cols], v[:, cols], og_t[:], s2_sq[:, cols], MULT, MULT)
+        rest = []
         for h in halves:
-            nc.vector.tensor_tensor(res[:, jcols(h)], f1[:, jcols(h)], tb[:, jcols(h)], ADD)
-            queue = nc.sync if h == 0 else nc.scalar
-            queue.dma_start(out[:, jcols(h)], res[:, jcols(h)])
+            turned_ps = ps.tile([P, 2, P], F32, name=f"turned_ps{h}")
+            for b in range(2):
+                cols = piece(J, J // P, 2 * h + b)
+                nc.tensor.matmul(turned_ps[:, b, :], lhsT=base_t[:, cols], rhs=ident[:], is_transpose=True, start=True, stop=False)
+                nc.tensor.matmul(turned_ps[:, b, :], lhsT=square[:, cols], rhs=ident[:], is_transpose=True, start=False, stop=True)
+            turned = tile(f"turned{h}", [P, 2, P])
+            nc.scalar.copy(turned[:], turned_ps[:])
+            rest_ps = ps.tile([P, 2, P], F32, name=f"rest_ps{h}")
+            for b in range(2):
+                nc.tensor.transpose(rest_ps[:, b, :], turned[:, b, :], ident[:])
+            rest.append(rest_ps[:].rearrange("p b n -> p (b n)"))
+        result = tile("result", [P, J])
+        for h, queue in enumerate((nc.sync, nc.scalar)):
+            cols = slot_half(h)
+            nc.vector.tensor_tensor(result[:, cols], linear[:, cols], rest[h], ADD)
+            queue.dma_start(out[:, cols], result[:, cols])

@@ -89,7 +89,7 @@ def tile_attend_gpcpickcentred_kernel(tc, tab_words, tab_scales, w1, gain, share
         dy_raw = tile("dy_raw", [P, PACK, M])
         nc.sync.dma_start(dy_raw[:], dy.rearrange("(p t) m -> p t m", t=PACK))
         gain_t = tile("gain_t", [P, 1])
-        nc.sync.dma_start(gain_t[:], gain)
+        nc.gpsimd.dma_start(gain_t[:], gain)
         offs2_t = tile("offs2_t", [P, M // LIST_ROWS], U16)
         nc.sync.dma_start(offs2_t[:], offs2)
         share_t = tile("share_t", [P, 1])
@@ -189,12 +189,13 @@ def tile_attend_gpcpickcentred_kernel(tc, tab_words, tab_scales, w1, gain, share
         for q in pick_parts:
             cols = pick_part(q)
             nc.vector.scalar_tensor_tensor(two_cs[:, cols], th[:, cols], 1.0, c0[:, cols], ADD, MULT)
-        cs_sums = group_sums("cs_sum", two_cs)
+        cs_sums = group_sums("cs_sum", two_cs, "sum_then_slope")
         for q in pick_parts:
             neg_centre(neg_two_ds, two_cs, cs_sums, q)
         nc.vector.tensor_tensor(s2[:].indirect(offs2_t[:]), neg_two_ds[:], neg_half[:], MULT)
         s2_sq = tile("s2_sq", [P, J])
-        nc.scalar.activation(s2_sq[:], s2[:], ACT.Square)
+        for h in halves:
+            nc.scalar.activation(s2_sq[:, slot_half(h)], s2[:, slot_half(h)], ACT.Square)
 
         hs2 = tile("hs2", [P, J])
         nc.vector.tensor_tensor(hs2[:], s2[:], two_gu2[:], MULT)
@@ -204,7 +205,7 @@ def tile_attend_gpcpickcentred_kernel(tc, tab_words, tab_scales, w1, gain, share
         hds_sums = group_sums("hds_sum", hds)
         for q in pick_parts:
             neg_centre(neg_ch, hds, hds_sums, q)
-        neg_four_slope = tile("neg_four_slope", [P, M])
+        neg_four_slope = tile("neg_four_slope", [P, M], F32, "sum_then_slope")
         for h in halves:
             cols = pick_half(h)
             nc.vector.scalar_tensor_tensor(neg_four_slope[:, cols], th[:, cols], -1.0, two_cs[:, cols], ADD, MULT)

import math
from contextlib import ExitStack

import concourse.mybir as mybir
from concourse.masks import make_identity

F32 = mybir.dt.float32
BF16 = mybir.dt.bfloat16
I32 = mybir.dt.int32
U32 = mybir.dt.uint32
U16 = mybir.dt.uint16
U8 = mybir.dt.uint8
FP8X4 = mybir.dt.float8_e4m3fn_x4
FP4X4 = mybir.dt.float4_e2m1fn_x4
ACT = mybir.ActivationFunctionType
MULT = mybir.AluOpType.mult
ADD = mybir.AluOpType.add
SUB = mybir.AluOpType.subtract
AXIS_X = mybir.AxisListType.X

P = 128
PACK = 4
K, R, F, T, J, M = 512, 128, 512, 2048, 512, 256
GROUP = 8
LIST_ROWS = 16
SCALE_ROWS = 16
QUADRANT = 32
LINE = 4
PICK_PARTS = 4
SLOT_PARTS = 4

FLOPS = 2 * K * R * J + 2 * F * R * M


def tile_attend_gpcpickcentred_kernel(tc, tab_words, tab_scales, w1, gain, share, pb, wo, dy, og, base, offs, offs2, out):
    nc = tc.nc
    halves = range(2)
    pick_parts = range(PICK_PARTS)
    slot_parts = range(SLOT_PARTS)
    part_groups = M // PICK_PARTS // GROUP

    def piece(width, count, i):
        return slice(i * width // count, (i + 1) * width // count)

    def slot_half(h):
        return piece(J, 2, h)

    def slot_part(q):
        return piece(J, SLOT_PARTS, q)

    def pick_half(h):
        return piece(M, 2, h)

    def pick_part(q):
        return piece(M, PICK_PARTS, q)

    with ExitStack() as ctx:
        sb = ctx.enter_context(tc.tile_pool(name="sb", bufs=1))
        ps = ctx.enter_context(tc.psum_pool(name="ps", bufs=1))

        def tile(name, shape, dtype=F32, tag=""):
            return sb.tile(shape, dtype, name=name, tag=tag, align_bytes=64)

        scales_t = tile("scales_t", [P, T], U8, "scales_then_dy")
        nc.vector.memset(scales_t[:].bitcast(I32), 0)
        ident = tile("ident", [P, P])
        nc.vector.memset(ident[:], 0.0)
        s2 = tile("s2", [P, J])
        nc.vector.memset(s2[:], 0.0)
        s53 = tile("s53", [P, J])
        nc.vector.memset(s53[:], 0.0)
        neg_half = tile("neg_half", [P, M])
        nc.vector.memset(neg_half[:], -0.5)
        make_identity(nc, ident[:], nomemset=True)

        offs_t = tile("offs_t", [P, J // LIST_ROWS], U16)
        nc.sync.dma_start(offs_t[:], offs)
        words_t = tile("words_t", [P, T], U16)
        nc.sync.dma_start(words_t[:].bitcast(I32), tab_words[0].bitcast(I32))
        w1_raw = tile("w1_raw", [P, PACK, R])
        nc.sync.dma_start(w1_raw[:], w1.rearrange("(p t) r -> p t r", t=PACK))
        scale_rows = tab_scales[0].bitcast(I32)
        for i in range(4):
            nc.sync.dma_start(scales_t[:].bitcast(I32)[i:P:QUADRANT, :], scale_rows[i:SCALE_ROWS:4, :])
        pb_pairs = tile("pb_pairs", [P, 2], F32, "pb_then_w1_then_wo")
        nc.scalar.dma_start(pb_pairs[:], pb[0].rearrange("(p c) -> p c", c=2))
        wo_raw = tile("wo_raw", [P, PACK, R], F32, "wo_then_h0")
        nc.sync.dma_start(wo_raw[:], wo.rearrange("(p t) r -> p t r", t=PACK))
        dy_raw = tile("dy_raw", [P, PACK, M])
        nc.sync.dma_start(dy_raw[:], dy.rearrange("(p t) m -> p t m", t=PACK))
        gain_t = tile("gain_t", [P, 1])
        nc.gpsimd.dma_start(gain_t[:], gain)
        offs2_t = tile("offs2_t", [P, M // LIST_ROWS], U16)
        nc.sync.dma_start(offs2_t[:], offs2)
        share_t = tile("share_t", [P, 1])
        nc.sync.dma_start(share_t[:], share)
        og_t = tile("og_t", [P, 1])
        nc.sync.dma_start(og_t[:], og)
        base_t = tile("base_t", [P, J])
        nc.sync.dma_start(base_t[:], base)

        def interleave(copy, dst, raw):
            copy(dst.rearrange("p (c i) t -> p c t i", i=LINE), raw.rearrange("p t (c i) -> p c t i", i=LINE))

        def scalar_cast(dst, src):
            nc.scalar.activation(dst, src, ACT.Copy)

        def quantize(name, interleaved, codes_tag="", scales_tag=""):
            width = interleaved.shape[1]
            codes = tile(name + "_codes", [P, width], U32, codes_tag)
            scales = tile(name + "_scales", [P, width], U8, scales_tag)
            nc.vector.quantize_mx(codes[:].bitcast(FP8X4), scales[:], interleaved.rearrange("p w t -> p (w t)"))
            return codes, scales

        def by_group(ap):
            return ap.rearrange("p (g e) -> p g e", e=GROUP)

        def spread(sums):
            return sums[:].rearrange("p (g o) -> p g o", o=1).to_broadcast([P, part_groups, GROUP])

        def group_sums(name, x, last_tag=""):
            sums = []
            for q in pick_parts:
                part = tile(f"{name}{q}", [P, part_groups], F32, last_tag if q == PICK_PARTS - 1 else "")
                nc.vector.tensor_reduce(part[:], by_group(x[:, pick_part(q)]), AXIS_X, ADD)
                sums.append(part)
            return sums

        def neg_centre(dst, x, sums, q):
            cols = pick_part(q)
            nc.vector.scalar_tensor_tensor(by_group(dst[:, cols]), spread(sums[q]), share8[:], by_group(x[:, cols]), MULT, SUB)

        slot_list = [offs_t[:, piece(J // LIST_ROWS, 2, h)] for h in halves]
        pick_list = [offs2_t[:, piece(M // LIST_ROWS, 2, h)] for h in halves]
        g_words = tile("g_words", [P, J], U16, "words_then_gain")
        nc.vector.tensor_copy(g_words[:], words_t[:].indirect(offs_t[:]))
        w1_bf = tile("w1_bf", [P, R, PACK], BF16, "w1_then_scales")
        interleave(scalar_cast, w1_bf[:], w1_raw[:])

        pb_ps = ps.tile([P, 2, P], F32, name="pb_ps")
        for c in range(2):
            nc.tensor.transpose(pb_ps[:, c, :], pb_pairs[:, c:c + 1].to_broadcast([P, P]), ident[:])
        pb_all = tile("pb_all", [P, M])
        nc.scalar.copy(pb_all[:].rearrange("p (n c) -> p n c", c=2), pb_ps[:].rearrange("p c n -> p n c"))

        g_scales = [tile("g_scales0", [P, J // 2], U8), tile("g_scales1", [P, J // 2], U8, "w1_then_scales")]
        nc.vector.tensor_copy(g_scales[0][:], scales_t[:].indirect(slot_list[0]))
        w1_codes, w1_scales = quantize("w1", w1_bf[:], "pb_then_w1_then_wo", "w1_then_share")
        nc.vector.tensor_copy(g_scales[1][:], scales_t[:].indirect(slot_list[1]))

        wo_bf = tile("wo_bf", [P, R, PACK], BF16)
        interleave(scalar_cast, wo_bf[:], wo_raw[:])
        h0 = tile("h0", [P, J], F32, "wo_then_h0")
        h1 = tile("h1", [P, J])
        for h in halves:
            a_ps = ps.tile([P, J // 2], F32, name=f"a_ps{h}")
            nc.tensor.matmul_mx(a_ps[:], lhsT=w1_codes[:].bitcast(FP8X4), lhsT_scale=w1_scales[:],
                                rhs=g_words[:, slot_half(h)].bitcast(FP4X4), rhs_scale=g_scales[h][:], start=True, stop=True)
            nc.scalar.activation(h0[:, slot_half(h)], a_ps[:], ACT.Tanh)
        neg_gain = tile("neg_gain", [P, 1], F32, "words_then_gain")
        nc.scalar.activation(neg_gain[:], gain_t[:], ACT.Copy, scale=-1.0)
        dy_bf = tile("dy_bf", [P, M, PACK], BF16, "scales_then_dy")
        for h in halves:
            nc.vector.tensor_scalar(h1[:, slot_half(h)], h0[:, slot_half(h)], gain_t[:], None, MULT)
        interleave(nc.vector.tensor_copy, dy_bf[:], dy_raw[:])
        dy_codes, dy_scales = quantize("dy", dy_bf[:])
        wo_codes, wo_scales = quantize("wo", wo_bf[:], "pb_then_w1_then_wo")
        c0 = ps.tile([P, M], F32, name="c0")
        nc.tensor.matmul_mx(c0[:], lhsT=wo_codes[:].bitcast(FP8X4), lhsT_scale=wo_scales[:],
                            rhs=dy_codes[:].bitcast(FP8X4), rhs_scale=dy_scales[:], start=True, stop=True)

        s, neg_z, th, two_cs, neg_two_ds = (tile(n, [P, M]) for n in ("s", "neg_z", "th", "two_cs", "neg_two_ds"))
        for h in halves:
            nc.vector.tensor_tensor(s[:, pick_half(h)], h1[:].indirect(pick_list[h]), pb_all[:, pick_half(h)], ADD)
        s_sums = group_sums("s_sum", s, "sum_then_v")
        share8 = tile("share8", [P, 1], F32, "w1_then_share")
        nc.vector.tensor_scalar(share8[:], share_t[:], 1.0 / GROUP, None, MULT)
        for q in pick_parts:
            neg_centre(neg_z, s, s_sums, q)
            nc.scalar.activation(th[:, pick_part(q)], neg_z[:, pick_part(q)], ACT.Tanh, scale=-0.5)

        h0_sq = tile("h0_sq", [P, J])
        nc.scalar.activation(h0_sq[:], h0[:], ACT.Square)
        gain_u = tile("gain_u", [P, J])
        nc.scalar.activation(gain_u[:], h0_sq[:], ACT.Identity, bias=gain_t[:], scale=neg_gain[:])
        two_gu2 = tile("two_gu2", [P, J])
        nc.scalar.activation(two_gu2[:], gain_u[:], ACT.Square, scale=math.sqrt(2.0))

        for q in pick_parts:
            cols = pick_part(q)
            nc.vector.scalar_tensor_tensor(two_cs[:, cols], th[:, cols], 1.0, c0[:, cols], ADD, MULT)
        cs_sums = group_sums("cs_sum", two_cs, "sum_then_slope")
        for q in pick_parts:
            neg_centre(neg_two_ds, two_cs, cs_sums, q)
        nc.vector.tensor_tensor(s2[:].indirect(offs2_t[:]), neg_two_ds[:], neg_half[:], MULT)
        s2_sq = tile("s2_sq", [P, J])
        for h in halves:
            nc.scalar.activation(s2_sq[:, slot_half(h)], s2[:, slot_half(h)], ACT.Square)

        hs2 = tile("hs2", [P, J])
        nc.vector.tensor_tensor(hs2[:], s2[:], two_gu2[:], MULT)
        hds, neg_ch, curved, r52 = (tile(n, [P, M]) for n in ("hds", "neg_ch", "curved", "r52"))
        for h in halves:
            nc.vector.tensor_copy(hds[:, pick_half(h)], hs2[:].indirect(pick_list[h]))
        hds_sums = group_sums("hds_sum", hds)
        for q in pick_parts:
            neg_centre(neg_ch, hds, hds_sums, q)
        neg_four_slope = tile("neg_four_slope", [P, M], F32, "sum_then_slope")
        for h in halves:
            cols = pick_half(h)
            nc.vector.scalar_tensor_tensor(neg_four_slope[:, cols], th[:, cols], -1.0, two_cs[:, cols], ADD, MULT)
        for q in pick_parts:
            cols = pick_part(q)
            nc.vector.scalar_tensor_tensor(curved[:, cols], neg_ch[:, cols], 0.25, neg_four_slope[:, cols], MULT, MULT)
        curved_sums = group_sums("curved_sum", curved)
        for q in pick_parts:
            nc.vector.tensor_scalar(by_group(r52[:, pick_part(q)]), spread(curved_sums[q]), share_t[:], -1.0 / GROUP, MULT, MULT)
        nc.vector.tensor_tensor(s53[:].indirect(offs2_t[:]), curved[:], r52[:], ADD)

        linear = tile("linear", [P, J])
        for h in halves:
            cols = slot_half(h)
            nc.vector.scalar_tensor_tensor(linear[:, cols], s53[:, cols], og_t[:], gain_u[:, cols], MULT, MULT)
        v = tile("v", [P, J], F32, "sum_then_v")
        for q in slot_parts:
            cols = slot_part(q)
            nc.vector.scalar_tensor_tensor(v[:, cols], h0[:, cols], -2.0, two_gu2[:, cols], MULT, MULT)
        square = tile("square", [P, J])
        for q in slot_parts:
            cols = slot_part(q)
            nc.vector.scalar_tensor_tensor(square[:, cols], v[:, cols], og_t[:], s2_sq[:, cols], MULT, MULT)
        rest = []
        for h in halves:
            turned_ps = ps.tile([P, 2, P], F32, name=f"turned_ps{h}")
            for b in range(2):
                cols = piece(J, J // P, 2 * h + b)
                nc.tensor.matmul(turned_ps[:, b, :], lhsT=base_t[:, cols], rhs=ident[:], is_transpose=True, start=True, stop=False)
                nc.tensor.matmul(turned_ps[:, b, :], lhsT=square[:, cols], rhs=ident[:], is_transpose=True, start=False, stop=True)
            turned = tile(f"turned{h}", [P, 2, P])
            nc.scalar.copy(turned[:], turned_ps[:])
            rest_ps = ps.tile([P, 2, P], F32, name=f"rest_ps{h}")
            for b in range(2):
                nc.tensor.transpose(rest_ps[:, b, :], turned[:, b, :], ident[:])
            rest.append(rest_ps[:].rearrange("p b n -> p (b n)"))
        result = tile("result", [P, J])
        for h, queue in enumerate((nc.sync, nc.scalar)):
            cols = slot_half(h)
            nc.vector.tensor_tensor(result[:, cols], linear[:, cols], rest[h], ADD)
            queue.dma_start(out[:, cols], result[:, cols])
